import numpy as np, ml_dtypes
CORES = [25,29,65,69,153,157,193,197]
N = 8
import mx_ref
BF = ml_dtypes.bfloat16
def entries(a):
    return np.ascontiguousarray(a.T).reshape(-1)
def table(e):
    return np.ascontiguousarray(np.reshape(e, (-1, 16)).T).astype(np.int32)
def cols(t, e):
    v = np.concatenate([t.reshape(128, -1, 4), np.zeros((128, 1, 4), BF)], axis=1)
    return np.ascontiguousarray(v[:, e]).reshape(128, -1)
def f(rng, *shape):
    return mx_ref.flush((rng.standard_normal(shape, dtype=np.float32) * np.exp2(rng.integers(-2, 3, shape[:-1] + (1,)))).astype(BF))
def wide(rng, *shape, cols=0):
    v = rng.standard_normal(shape, dtype=np.float32) * np.exp2(rng.integers(-12, 13, shape)).astype(np.float32)
    if cols: v *= np.repeat(np.exp2(rng.integers(-cols, cols + 1, shape[:-2] + (1, shape[-1] // 4))) * (rng.random(shape[:-2] + (1, shape[-1] // 4)) > 0.0625), 4, axis=-1).astype(np.float32)
    return mx_ref.flush(v.astype(BF))
T, W, UN, CR = 1024, 768, 320, 128
HOST = [0 if k < 128 else 1 for k in CORES]
def lists(rng, full=False, alike=False):
    uni, need, pos = np.full((N, 2, UN), -1), np.full((N, N, CR), -1), []
    for q in range(N):
        for g in range(2):
            mates = [r for r in range(N) if HOST[r] == g]
            n = UN if full else int(rng.integers(CR >> 1, CR + 1)) if alike else int(rng.integers(UN >> 2, UN + 1))
            at = rng.permutation(UN)[:n]
            uni[q, g, at] = rng.permutation(T)[:n]
            who = rng.permutation(np.repeat(np.arange(len(mates)), CR))[:n]
            for i, r in enumerate(mates):
                e, others = at[who == i], at[who != i]
                if alike: e = at
                else:
                    k = CR if full else int(rng.integers(max(len(e), CR >> 2), min(CR, n) + 1))
                    e = np.concatenate([e, rng.permutation(others)[:k - len(e)]])
                need[r, q, rng.permutation(CR)[:len(e)]] = e
    for r in range(N):
        ok = np.flatnonzero(need[r].reshape(-1) >= 0)
        pos.append(table(rng.permutation(ok)[:W] if full else rng.choice(ok, W)))
    return {"uni": np.stack([table(e.reshape(-1)) for e in uni]), "need": np.stack([table(e.reshape(-1)) for e in need]), "pos": np.stack(pos)}
def setup_inputs(rng):
    return {"c": f(rng, N, 128, 4 * T), "w": f(rng, N, 128, 512), **lists(rng)}
def setup_inputs_alike(rng):
    return {**setup_inputs(rng), **lists(rng, alike=True)}
def setup_inputs_pairs(rng):
    d = setup_inputs(rng)
    uni, need = np.full((N, 2, UN), -1), np.full((N, N, CR), -1)
    for g in range(2):
        mates = rng.permutation([r for r in range(N) if HOST[r] == g])
        for q in range(N):
            at = rng.permutation(UN)[:2 * CR]
            uni[q, g, at] = rng.permutation(T)[:2 * CR]
            for i, r in enumerate(mates):
                need[r, q] = rng.permutation(at[:CR] if i < len(mates) // 2 else at[CR:])
    pos = [table(rng.choice(N * CR, W)) for r in range(N)]
    return {**d, "uni": np.stack([table(e.reshape(-1)) for e in uni]), "need": np.stack([table(e.reshape(-1)) for e in need]), "pos": np.stack(pos)}
def setup_inputs_full(rng):
    return {**setup_inputs(rng), **lists(rng, full=True)}
def setup_inputs_few(rng):
    d = {**setup_inputs(rng), **lists(rng, full=True)}
    uni = np.stack([entries(e) for e in d["uni"]]).reshape(N, 2, UN)
    need = np.stack([entries(e) for e in d["need"]]).reshape(N, N, CR)
    pos = [None] * N
    for g in range(2):
        p = rng.permutation(N)
        h = [HOST[q] for q in p]
        lead = [h.index(0), h.index(1)]
        own = np.concatenate([p[lead], np.delete(p, lead)])[:-(-W // CR)]
        rest = np.setdiff1d(np.arange(N), own)
        uni[rest, g] = -1
        for r in range(N):
            if HOST[r] != g: continue
            need[r, rest] = -1
            s = rng.permutation(own)[:, None] * CR + np.arange(CR)
            s[-1] = rng.permutation(s[-1])
            pos[r] = table(rng.permutation(s.reshape(-1)[:W]))
    return {**d, "uni": np.stack([table(e.reshape(-1)) for e in uni]), "need": np.stack([table(e.reshape(-1)) for e in need]), "pos": np.stack(pos)}
def setup_inputs_spread(rng):
    d = setup_inputs(rng); d["c"] = wide(rng, N, 128, 4 * T, cols=6); return d
def check_inputs(d):
    b = []
    uni = np.stack([entries(e) for e in d["uni"]]).reshape(N, 2, UN)
    need = np.stack([entries(e) for e in d["need"]]).reshape(N, N, CR)
    if uni.min() < -1 or uni.max() >= T: b.append("uni")
    if need.min() < -1 or need.max() >= UN: return b + ["need"]
    for q in range(N):
        for g in range(2):
            e = uni[q, g][uni[q, g] >= 0]
            if len(set(e.tolist())) != len(e): b.append("a column of one owner twice for one host")
            named = set()
            for r in range(N):
                if HOST[r] != g: continue
                k = need[r, q][need[r, q] >= 0]
                if len(set(k.tolist())) != len(k): b.append("need names an entry of one union twice")
                if (uni[q, g][k] < 0).any(): b.append("need names an empty entry of uni")
                named |= set(k.tolist())
            if set(np.flatnonzero(uni[q, g] >= 0).tolist()) - named: b.append("an entry of uni that no rank of the host needs")
    for r in range(N):
        p = entries(d["pos"][r])
        if p.min() < 0 or p.max() >= N * CR or (need[r].reshape(-1)[p] < 0).any(): b.append("pos")
    return b
def reference(c, w, uni, need, pos):
    uni = np.stack([entries(e) for e in uni]).reshape(N, 2, UN)
    need = np.stack([entries(e) for e in need]).reshape(N, N, CR)
    y = np.zeros((N, 128, W), np.float32)
    for r in range(N):
        g = HOST[r]
        t = np.concatenate([cols(c[q], np.where(need[r, q] >= 0, uni[q, g][need[r, q]], -1)) for q in range(N)], axis=1)
        y[r] = mx_ref.matmul(mx_ref.quantize(w[r]), mx_ref.quantize(cols(t, entries(pos[r]))))
    return {"y": y}

@@ -1,0 +1,261 @@
+from concourse.bass import DstId, RemoteDMATransfer
+from concourse.mybir import dt, AluOpType, ActivationFunctionType
+
+COPY = ActivationFunctionType.Copy
+TC, W, UN, CR, N = 1024, 768, 320, 128, 8
+F8, U8 = "float8_e4m3fn_x4", "uint8"
+UO, LO = UN // 16, CR // 16
+CHUNKS = [(0, 384), (384, 768), (768, 1024)]
+PIECES = [(0, 160), (160, 320)]
+YP = [(0, 160), (416, 576), (160, 416), (576, 768)]
+
+SCRATCH = {
+    "cb": ("sbuf", [128, 4 * TC], "bfloat16"), "wb": ("sbuf", [128, 512], "bfloat16"),
+    "ui": ("sbuf", [128, 2 * UO], "int32"), "ni": ("sbuf", [128, N * LO], "int32"), "pi": ("sbuf", [128, W // 16], "int32"),
+    "uo": ("sbuf", [128, 2 * UO], "uint16"), "no": ("sbuf", [128, N * LO], "uint16"), "po": ("sbuf", [128, W // 16], "uint16"),
+    "nbo": ("sbuf", [128, 3 * LO], "uint16"),
+    "mo": ("sbuf", [128, 2 * LO], "uint16"),
+    "ln": ("sbuf", [128, 3 * LO], "uint16"),
+    "lx": ("sbuf", [128, 2 * LO], "uint16"),
+    "lh": ("sbuf", [128, LO], "uint16"),
+    "z": ("sbuf", [128, N * CR], "float32"), "yo": ("sbuf", [128, W], "float32"),
+    "ps": ("psum", [128, 512 * 7], "float32"),
+}
+for _n, _w in [("c", TC), ("w", 128),
+               ("u", UN), ("v", UN),
+               ("x", UN), ("h", CR),
+               ("r", 2 * UN),
+               ("e", 2 * CR), ("ek", 2 * CR),
+               ("n", CR), ("f", CR),
+               ("s", CR),
+               ("l", 2 * CR), ("t", 2 * CR),
+               ("m", 2 * CR)]:
+    SCRATCH[_n + "q"] = ("sbuf", [128, _w], F8)
+    SCRATCH[_n + "p"] = ("sbuf", [128, _w], U8)
+
+PICKS = ["u0", "u1", "v", "n", "e", "s", "l", "m"]
+SEMAPHORES = (["c0", "c1", "c2", "wl", "ul", "nl", "pl", "k_no", "k_nbo", "k_mo", "k_uo", "k_po", "qc", "qw", "sent", "ystore",
+               "a_lh", "a_ln", "a_lx", "zv", "zs"]
+              + [a + b for a in ("a_x", "a_h", "a_r", "a_ek", "a_f", "a_t") for b in "qp"]
+              + ["p_" + a + b for a in PICKS for b in "qp"]
+              + ["mm%d" % i for i in range(7)] + ["g%d" % i for i in range(len(YP))])
+
+
+def _mask(engines):
+    m = 0
+    for e in engines:
+        m |= 1 << e
+    return m
+
+
+def _rel(topo, cores, r):
+    c = cores[r]
+    here = [k for k in range(N) if topo.host(cores[k]) == topo.host(c)]
+    there = [k for k in range(N) if topo.host(cores[k]) != topo.host(c) and topo.die(cores[k]) == topo.die(c)]
+    nb = [k for k in here if k != r and topo.chip(cores[k]) == topo.chip(c)][0]
+    cross = [k for k in here if topo.chip(cores[k]) != topo.chip(c)]
+    twin = [k for k in there if topo.chip(cores[k]) == topo.chip(c)][0]
+    other = [k for k in there if k != twin][0]
+    return nb, cross, twin, other
+
+
+def _hands(topo, cores, r):
+    c = cores[r]
+    far = cores[_rel(topo, cores, r)[1][0]]
+    return [k for k in topo.cores_of(c) if k != c and topo.die(k) == topo.die(c) and topo.may_write(k, far)][:2]
+
+
+def _view(t, s, a, b):
+    return t[:, a:b].bitcast(dt.uint8) if s == "q" else t[:, a:b]
+
+
+def _caller(g, core, T, topo):
+    sent = [0]
+
+    def call(jobs):
+        if len(jobs) == 1:
+            d, out, src, sem, eng = jobs[0]
+            rid, pid = topo.addr(d, core)
+            g.remote_dma(out, src, sem, T.sem.sent, pid, rid, _mask(eng))
+        else:
+            tr = []
+            for d, out, src, sem, eng in jobs:
+                rid, pid = topo.addr(d, core)
+                tr.append(RemoteDMATransfer(dst_ids=[DstId(rid=rid, pnc=pid)], dma_engine_mask=_mask(eng), remote_sem=sem,
+                                            srcs=[src], dsts=[out]))
+            g.remote_dma_fused(tr, local_sem=T.sem.sent)
+        sent[0] += sum(len(j[4]) for j in jobs)
+
+    return call, sent
+
+
+def _hand_program(g, core, T, topo, r, i):
+    cores, S = T.cores, T.sem
+    me = cores[r]
+    nb, cross, twin, other = _rel(topo, cores, r)
+    call, sent = _caller(g, core, T, topo)
+    d = cores[cross[i]]
+    far = [cores[k] for k in cross if topo.die(cores[k]) == topo.die(me)][0]
+    away = topo.engines(core, far)
+    near = [e for e in topo.engines(core, me) if e not in away]
+    slot = _rel(topo, cores, cross[i])[1].index(r)
+    g.wait_ge(S.a_lh, len(away) // 2)
+    call([(d, T.lx[:, slot * LO:(slot + 1) * LO], T.lh[:], S.a_lx, away)])
+    a, b = PIECES[i]
+    for s in "qp":
+        g.wait_ge(S["a_x" + s], len(away))
+        src = _view(T["x" + s], s, a, b)
+        call([(far, _view(T["r" + s], s, UN + a, UN + b), src, S["a_r" + s], away),
+              (me, _view(T["r" + s], s, a, b), src, S["a_r" + s], near)])
+    for s in "qp":
+        g.wait_ge(S["a_h" + s], len(topo.engines(me, core)) // 2)
+        call([(d, _view(T["ek" + s], s, slot * CR, (slot + 1) * CR), _view(T["h" + s], s, 0, CR), S["a_ek" + s], away)])
+    g.wait_ge(S.sent, sent[0])
+
+
+def rank_program(g, core, T, topo):
+    rank = T.rank_of(core)
+    cores = T.cores
+    if rank is None:
+        for r in range(N):
+            hands = _hands(topo, cores, r)
+            if core in hands:
+                _hand_program(g, core, T, topo, r, hands.index(core))
+        return
+    v, sc, te, sy = g.vector, g.scalar, g.tensor, g.sync
+    S = T.sem
+    nb, cross, twin, other = _rel(topo, cores, rank)
+    nbrel = _rel(topo, cores, nb)
+    hands = _hands(topo, cores, rank)
+    away = _hands(topo, cores, twin)
+    host = 0 if topo.host(core) == topo.host(cores[0]) else 1
+    leave = topo.engines(core, cores[twin])
+    chip = topo.engines(core, cores[nb])
+    half = len(leave) // 2
+
+    for k in range(4):
+        sy.dma_start(T.ni[16 * k:16 * k + 16, :], T.need[:]).then_inc(S.nl, 16)
+        sc.dma_start(T.ni[16 * (k + 4):16 * (k + 4) + 16, :], T.need[:]).then_inc(S.nl, 16)
+    for i, (a, b) in enumerate(CHUNKS):
+        if i == len(CHUNKS) - 1:
+            for k in range(4):
+                sy.dma_start(T.ui[16 * k:16 * k + 16, :], T.uni[:]).then_inc(S.ul, 16)
+                sc.dma_start(T.ui[16 * (k + 4):16 * (k + 4) + 16, :], T.uni[:]).then_inc(S.ul, 16)
+        sy.dma_start(T.cb[:, 4 * a:4 * b], T.c[:, 4 * a:4 * b]).then_inc(S["c%d" % i], 16)
+    sy.wait_ge(S.c1, 16)
+    sy.dma_start(T.wb[:], T.w[:]).then_inc(S.wl, 16)
+    for k in range(8):
+        sy.dma_start(T.pi[16 * k:16 * k + 16, :], T.pos[:]).then_inc(S.pl, 16)
+
+    def pick(name, out, a, b, win, offs, waits=(), own=()):
+        for s, n in waits:
+            v.wait_ge(S[s], n)
+            sc.wait_ge(S[s], n)
+        for s, n in own:
+            v.wait_ge(S[s + "q"], n)
+            sc.wait_ge(S[s + "p"], n)
+        v.tensor_copy(T[out + "q"][:, a:b].bitcast(dt.uint32), T[win + "q"][:].bitcast(dt.uint32).indirect(offs)).then_inc(S["p_" + name + "q"], 1)
+        sc.activation(T[out + "p"][:, a:b], T[win + "p"][:].indirect(offs), COPY).then_inc(S["p_" + name + "p"], 1)
+
+    def offsets(out, at, q, add, sem):
+        o, i = out[:, at * LO:(at + 1) * LO], T.ni[:, q * LO:(q + 1) * LO]
+        if add:
+            v.tensor_scalar(o, i, 0, add, AluOpType.max, AluOpType.add).then_inc(sem, 1)
+        else:
+            v.tensor_copy(o, i).then_inc(sem, 1)
+
+    v.wait_ge(S.nl, 128)
+    v.tensor_copy(T.no[:], T.ni[:]).then_inc(S.k_no, 1)
+    offsets(T.nbo, 0, nb, 0, S.k_nbo)
+    offsets(T.nbo, 1, nbrel[2], 0, S.k_nbo)
+    offsets(T.nbo, 2, nbrel[3], UN, S.k_nbo)
+    offsets(T.mo, 0, twin, 0, S.k_mo)
+    offsets(T.mo, 1, other, UN, S.k_mo)
+    for i, (a, b) in enumerate(CHUNKS):
+        v.wait_ge(S["c%d" % i], 16)
+        v.quantize_mx(T.cq[:, a:b], T.cp[:, a:b], T.cb[:, 4 * a:4 * b]).then_inc(S.qc, 1)
+        if i == 1:
+            v.wait_ge(S.ul, 128)
+            v.tensor_copy(T.uo[:], T.ui[:]).then_inc(S.k_uo, 1)
+    far, own = (1 - host) * UO, host * UO
+    for i, (a, b) in enumerate(PIECES):
+        pick("u%d" % i, "u", a, b, "c", T.uo[:, far + a // 16:far + b // 16], [("qc", len(CHUNKS)), ("k_uo", 1)] if i == 0 else [])
+    pick("v", "v", 0, UN, "c", T.uo[:, own:own + UO])
+    pick("n", "n", 0, CR, "v", T.ln[:, 0:LO], [("a_ln", len(leave))], [("p_v", 1)])
+    pick("e", "e", 0, 2 * CR, "v", T.lx[:], [("a_lx", 2 * len(leave))])
+    pick("s", "s", 0, CR, "v", T.no[:, rank * LO:(rank + 1) * LO], [("k_no", 1)])
+    v.wait_ge(S.wl, 16)
+    v.quantize_mx(T.wq[:], T.wp[:], T.wb[:]).then_inc(S.qw, 1)
+    v.wait_ge(S.pl, 128)
+    v.tensor_copy(T.po[:], T.pi[:]).then_inc(S.k_po, 1)
+    pick("l", "l", 0, 2 * CR, "r", T.ln[:, LO:3 * LO], [], [("a_r", 4 * len(leave))])
+    pick("m", "m", 0, 2 * CR, "r", T.mo[:], [("k_mo", 2)])
+
+    call, sent = _caller(g, core, T, topo)
+    g.wait_ge(S.k_no, 1)
+    call([(hands[i], T.lh[:], T.no[:, q * LO:(q + 1) * LO], S.a_lh, leave[i * half:(i + 1) * half]) for i, q in enumerate(cross)])
+    g.wait_ge(S.k_nbo, 3)
+    call([(cores[nb], T.ln[:], T.nbo[:], S.a_ln, leave)])
+    for s in "qp":
+        for i, (a, b) in enumerate(PIECES):
+            g.wait_ge(S["p_u%d%s" % (i, s)], 1)
+            call([(away[i], _view(T["x" + s], s, a, b), _view(T["u" + s], s, a, b), S["a_x" + s], leave)])
+
+    def columns(name, land, n):
+        for s in "qp":
+            g.wait_ge(S["p_" + name + s], 1)
+            call([(cores[nb], _view(T[land + s], s, 0, n), _view(T[name + s], s, 0, n), S["a_" + land + s], chip)])
+
+    columns("n", "f", CR)
+    for s in "qp":
+        g.wait_ge(S["p_e" + s], 1)
+        call([(hands[i], _view(T["h" + s], s, 0, CR), _view(T["e" + s], s, i * CR, (i + 1) * CR), S["a_h" + s],
+               chip[i * len(chip) // 2:(i + 1) * len(chip) // 2]) for i in range(2)])
+    columns("l", "t", 2 * CR)
+    g.wait_ge(S.sent, sent[0])
+
+    te.wait_ge(S.qw, 1)
+
+    def mm(i, name, a, b, waits=()):
+        for s, n in waits:
+            te.wait_ge(S[s], n)
+        te.matmul_mx(T.ps[:, 512 * i:512 * i + b - a], T.wq[:], T.wp[:], T[name + "q"][:, a:b], T[name + "p"][:, a:b], True, True).then_inc(S["mm%d" % i], 1)
+
+    mm(0, "s", 0, CR, [("p_sq", 1), ("p_sp", 1)])
+    mm(1, "f", 0, CR, [("a_fq", len(chip)), ("a_fp", len(chip))])
+    mm(2, "m", 0, 2 * CR, [("p_mq", 1), ("p_mp", 1)])
+    mm(3, "ek", 0, CR, [("a_ekq", 2 * len(leave)), ("a_ekp", 2 * len(leave))])
+    mm(4, "ek", CR, 2 * CR)
+    mm(5, "t", 0, CR, [("a_tq", len(chip)), ("a_tp", len(chip))])
+    mm(6, "t", CR, 2 * CR)
+
+    def zv(i, at, q):
+        v.wait_ge(S["mm%d" % i], 1)
+        v.tensor_copy(T.z[:, q * CR:(q + 1) * CR], T.ps[:, 512 * i + at * CR:512 * i + (at + 1) * CR]).then_inc(S.zv, 1)
+
+    def zs(i, at, q):
+        sc.wait_ge(S["mm%d" % i], 1)
+        sc.activation(T.z[:, q * CR:(q + 1) * CR], T.ps[:, 512 * i + at * CR:512 * i + (at + 1) * CR], COPY).then_inc(S.zs, 1)
+
+    zv(0, 0, rank)
+    zs(1, 0, nb)
+    zv(2, 0, twin)
+    zv(2, 1, other)
+    zv(3, 0, cross[0])
+    zs(4, 0, cross[1])
+    zv(5, 0, nbrel[2])
+    zs(6, 0, nbrel[3])
+    for q in (v, sc):
+        q.wait_ge(S.k_po, 1)
+        q.wait_ge(S.zv, 5)
+        q.wait_ge(S.zs, 3)
+    for i, (a, b) in enumerate(YP):
+        offs = T.po[:, a // 16:b // 16]
+        if i % 2 == 0:
+            v.tensor_copy(T.yo[:, a:b], T.z[:].indirect(offs)).then_inc(S["g%d" % i], 1)
+        else:
+            sc.activation(T.yo[:, a:b], T.z[:].indirect(offs), COPY).then_inc(S["g%d" % i], 1)
+    for i, (a, b) in enumerate(YP):
+        sy.wait_ge(S["g%d" % i], 1)
+        sy.dma_start(T.y[:, a:b], T.yo[:, a:b]).then_inc(S.ystore, 16)
+    sy.wait_ge(S.ystore, 16 * len(YP))

@@ -1,30 +1,30 @@
 from concourse.bass import DstId, RemoteDMATransfer
-from concourse.mybir import dt, AluOpType, ActivationFunctionType
+from concourse.mybir import dt, ActivationFunctionType
 
 COPY = ActivationFunctionType.Copy
-TC, W, UN, CR, N = 1024, 768, 320, 128, 8
+TC, W, UN, CR, N, WORLD = 1024, 768, 320, 128, 8, 256
 F8, U8 = "float8_e4m3fn_x4", "uint8"
 UO, LO = UN // 16, CR // 16
-CHUNKS = [(0, 384), (384, 768), (768, 1024)]
+CHUNKS = [(0, 512), (512, 896), (896, 1024)]
 PIECES = [(0, 160), (160, 320)]
-YP = [(0, 160), (416, 576), (160, 416), (576, 768)]
+HELD = (0, 1)
+YP = [(0, 64, 128), (128, 288, 448), (448, 608, 768)]
 
 SCRATCH = {
     "cb": ("sbuf", [128, 4 * TC], "bfloat16"), "wb": ("sbuf", [128, 512], "bfloat16"),
     "ui": ("sbuf", [128, 2 * UO], "int32"), "ni": ("sbuf", [128, N * LO], "int32"), "pi": ("sbuf", [128, W // 16], "int32"),
     "uo": ("sbuf", [128, 2 * UO], "uint16"), "no": ("sbuf", [128, N * LO], "uint16"), "po": ("sbuf", [128, W // 16], "uint16"),
     "nbo": ("sbuf", [128, 3 * LO], "uint16"),
-    "mo": ("sbuf", [128, 2 * LO], "uint16"),
     "ln": ("sbuf", [128, 3 * LO], "uint16"),
     "lx": ("sbuf", [128, 2 * LO], "uint16"),
     "lh": ("sbuf", [128, LO], "uint16"),
     "z": ("sbuf", [128, N * CR], "float32"), "yo": ("sbuf", [128, W], "float32"),
-    "ps": ("psum", [128, 512 * 7], "float32"),
+    "ps": ("psum", [128, 512 * N], "float32"),
 }
 for _n, _w in [("c", TC), ("w", 128),
                ("u", UN), ("v", UN),
                ("x", UN), ("h", CR),
-               ("r", 2 * UN),
+               ("r0", UN), ("r1", UN),
                ("e", 2 * CR), ("ek", 2 * CR),
                ("n", CR), ("f", CR),
                ("s", CR),
@@ -33,12 +33,13 @@ for _n, _w in [("c", TC), ("w", 128),
     SCRATCH[_n + "q"] = ("sbuf", [128, _w], F8)
     SCRATCH[_n + "p"] = ("sbuf", [128, _w], U8)
 
-PICKS = ["u0", "u1", "v", "n", "e", "s", "l", "m"]
-SEMAPHORES = (["c0", "c1", "c2", "wl", "ul", "nl", "pl", "k_no", "k_nbo", "k_mo", "k_uo", "k_po", "qc", "qw", "sent", "ystore",
-               "a_lh", "a_ln", "a_lx", "zv", "zs"]
-              + [a + b for a in ("a_x", "a_h", "a_r", "a_ek", "a_f", "a_t") for b in "qp"]
+PICKS = ["u0", "u1", "v", "n", "e0", "e1", "s", "l0", "l1", "m0", "m1"]
+SEMAPHORES = (["wl", "ul", "nl", "pl", "k_no", "k_nbo", "k_uo", "k_po", "qa", "qc", "qw", "sent", "ystore",
+               "a_lh", "a_ln", "a_lx0", "a_lx1", "zv", "zs", "a_k0", "a_k1"]
+              + ["c%d" % i for i in range(len(CHUNKS))]
+              + [a + b for a in ("a_x", "a_h", "a_r0", "a_r1", "a_f") for b in "qp"] + ["a_t0", "a_t1", "a_tp"]
               + ["p_" + a + b for a in PICKS for b in "qp"]
-              + ["mm%d" % i for i in range(7)] + ["g%d" % i for i in range(len(YP))])
+              + ["mm%d" % i for i in range(N)] + ["g%d" % i for i in range(len(YP))])
 
 
 def _mask(engines):
@@ -53,7 +54,7 @@ def _rel(topo, cores, r):
     here = [k for k in range(N) if topo.host(cores[k]) == topo.host(c)]
     there = [k for k in range(N) if topo.host(cores[k]) != topo.host(c) and topo.die(cores[k]) == topo.die(c)]
     nb = [k for k in here if k != r and topo.chip(cores[k]) == topo.chip(c)][0]
-    cross = [k for k in here if topo.chip(cores[k]) != topo.chip(c)]
+    cross = sorted((k for k in here if topo.chip(cores[k]) != topo.chip(c)), key=lambda k: topo.die(cores[k]) == topo.die(c))
     twin = [k for k in there if topo.chip(cores[k]) == topo.chip(c)][0]
     other = [k for k in there if k != twin][0]
     return nb, cross, twin, other
@@ -62,7 +63,8 @@ def _rel(topo, cores, r):
 def _hands(topo, cores, r):
     c = cores[r]
     far = cores[_rel(topo, cores, r)[1][0]]
-    return [k for k in topo.cores_of(c) if k != c and topo.die(k) == topo.die(c) and topo.may_write(k, far)][:2]
+    fit = [k for k in range(WORLD) if topo.die(k) == topo.die(c) and topo.may_write(k, far)]
+    return [[k for k in fit if topo.mates(k, far)][0], [k for k in fit if k in topo.cores_of(c)][0]]
 
 
 def _view(t, s, a, b):
@@ -94,22 +96,21 @@ def _hand_program(g, core, T, topo, r, i):
     me = cores[r]
     nb, cross, twin, other = _rel(topo, cores, r)
     call, sent = _caller(g, core, T, topo)
-    d = cores[cross[i]]
-    far = [cores[k] for k in cross if topo.die(cores[k]) == topo.die(me)][0]
+    far = cores[cross[1]]
     away = topo.engines(core, far)
-    near = [e for e in topo.engines(core, me) if e not in away]
-    slot = _rel(topo, cores, cross[i])[1].index(r)
+    near = [e for e in topo.engines(core, me) if e not in away] or away
     g.wait_ge(S.a_lh, len(away) // 2)
-    call([(d, T.lx[:, slot * LO:(slot + 1) * LO], T.lh[:], S.a_lx, away)])
-    a, b = PIECES[i]
-    for s in "qp":
+    call([(cores[cross[1 - i]], T.lx[:, (1 - i) * LO:(2 - i) * LO], T.lh[:], S["a_lx%d" % (1 - i)], away)])
+    for s, (a, b) in [("p", (0, UN))] * i + [("q", PIECES[i])]:
         g.wait_ge(S["a_x" + s], len(away))
         src = _view(T["x" + s], s, a, b)
-        call([(far, _view(T["r" + s], s, UN + a, UN + b), src, S["a_r" + s], away),
-              (me, _view(T["r" + s], s, a, b), src, S["a_r" + s], near)])
-    for s in "qp":
-        g.wait_ge(S["a_h" + s], len(topo.engines(me, core)) // 2)
-        call([(d, _view(T["ek" + s], s, slot * CR, (slot + 1) * CR), _view(T["h" + s], s, 0, CR), S["a_ek" + s], away)])
+        to_far = (far, _view(T["r1" + s], s, a, b), src, S["a_r1" + s], away)
+        to_me = (me, _view(T["r0" + s], s, a, b), src, S["a_r0" + s], near)
+        for part in ([[to_far, to_me]] if i else [[to_me], [to_far]]):
+            call(part)
+    for s, came in (("q", len(topo.engines(me, core))), ("p", len(away))):
+        g.wait_ge(S["a_h" + s], came)
+        call([(cores[cross[i]], _view(T["ek" + s], s, i * CR, (i + 1) * CR), _view(T["h" + s], s, 0, CR), S["a_k%d" % i], away)])
     g.wait_ge(S.sent, sent[0])
 
 
@@ -131,131 +132,136 @@ def rank_program(g, core, T, topo):
     host = 0 if topo.host(core) == topo.host(cores[0]) else 1
     leave = topo.engines(core, cores[twin])
     chip = topo.engines(core, cores[nb])
+    stay = [e for e in chip if e not in leave]
     half = len(leave) // 2
 
     for k in range(4):
-        sy.dma_start(T.ni[16 * k:16 * k + 16, :], T.need[:]).then_inc(S.nl, 16)
-        sc.dma_start(T.ni[16 * (k + 4):16 * (k + 4) + 16, :], T.need[:]).then_inc(S.nl, 16)
+        (sy, sc)[k % 2].dma_start(T.ni[16 * k:16 * k + 16, :], T.need[:]).then_inc(S.nl, 16)
     for i, (a, b) in enumerate(CHUNKS):
-        if i == len(CHUNKS) - 1:
-            for k in range(4):
-                sy.dma_start(T.ui[16 * k:16 * k + 16, :], T.uni[:]).then_inc(S.ul, 16)
-                sc.dma_start(T.ui[16 * (k + 4):16 * (k + 4) + 16, :], T.uni[:]).then_inc(S.ul, 16)
         sy.dma_start(T.cb[:, 4 * a:4 * b], T.c[:, 4 * a:4 * b]).then_inc(S["c%d" % i], 16)
-    sy.wait_ge(S.c1, 16)
-    sy.dma_start(T.wb[:], T.w[:]).then_inc(S.wl, 16)
+    for k in range(2):
+        sc.dma_start(T.ui[16 * k:16 * k + 16, :], T.uni[:]).then_inc(S.ul, 16)
     for k in range(8):
         sy.dma_start(T.pi[16 * k:16 * k + 16, :], T.pos[:]).then_inc(S.pl, 16)
+    sy.wait_ge(S.p_vq, 1)
+    sy.dma_start(T.wb[:], T.w[:]).then_inc(S.wl, 16)
 
-    def pick(name, out, a, b, win, offs, waits=(), own=()):
-        for s, n in waits:
-            v.wait_ge(S[s], n)
-            sc.wait_ge(S[s], n)
-        for s, n in own:
-            v.wait_ge(S[s + "q"], n)
-            sc.wait_ge(S[s + "p"], n)
-        v.tensor_copy(T[out + "q"][:, a:b].bitcast(dt.uint32), T[win + "q"][:].bitcast(dt.uint32).indirect(offs)).then_inc(S["p_" + name + "q"], 1)
-        sc.activation(T[out + "p"][:, a:b], T[win + "p"][:].indirect(offs), COPY).then_inc(S["p_" + name + "p"], 1)
+    def pick(name, out, a, b, win, offs, waits=(), own=(), sides="qp"):
+        for s in sides:
+            queue = v if s == "q" else sc
+            for sem, n in list(waits) + [(k + s, n) for k, n in own]:
+                queue.wait_ge(S[sem], n)
+            if s == "q":
+                made = v.tensor_copy(T[out + s][:, a:b].bitcast(dt.uint32), T[win + s][:].bitcast(dt.uint32).indirect(offs))
+            else:
+                made = sc.activation(T[out + s][:, a:b], T[win + s][:].indirect(offs), COPY)
+            made.then_inc(S["p_" + name + s], 1)
 
-    def offsets(out, at, q, add, sem):
-        o, i = out[:, at * LO:(at + 1) * LO], T.ni[:, q * LO:(q + 1) * LO]
-        if add:
-            v.tensor_scalar(o, i, 0, add, AluOpType.max, AluOpType.add).then_inc(sem, 1)
-        else:
-            v.tensor_copy(o, i).then_inc(sem, 1)
+    def spread(out, loaded, n, lsem, sem):
+        v.wait_ge(lsem, n)
+        for k in range(0, 128, n):
+            v.tensor_copy(out[k:k + n, :], loaded[0:n, :]).then_inc(sem, 1)
 
-    v.wait_ge(S.nl, 128)
-    v.tensor_copy(T.no[:], T.ni[:]).then_inc(S.k_no, 1)
-    offsets(T.nbo, 0, nb, 0, S.k_nbo)
-    offsets(T.nbo, 1, nbrel[2], 0, S.k_nbo)
-    offsets(T.nbo, 2, nbrel[3], UN, S.k_nbo)
-    offsets(T.mo, 0, twin, 0, S.k_mo)
-    offsets(T.mo, 1, other, UN, S.k_mo)
+    def zv(i, q):
+        v.wait_ge(S["mm%d" % i], 1)
+        v.tensor_copy(T.z[:, q * CR:(q + 1) * CR], T.ps[:, 512 * i:512 * i + CR]).then_inc(S.zv, 1)
+
+    def zs(i, q):
+        sc.wait_ge(S["mm%d" % i], 1)
+        sc.activation(T.z[:, q * CR:(q + 1) * CR], T.ps[:, 512 * i:512 * i + CR], COPY).then_inc(S.zs, 1)
+
+    spread(T.no, T.ni, 64, S.nl, S.k_no)
+    v.wait_ge(S.k_no, 2)
+    for at, q in enumerate((nb, nbrel[2], nbrel[3])):
+        v.tensor_copy(T.nbo[:, at * LO:(at + 1) * LO], T.no[:, q * LO:(q + 1) * LO]).then_inc(S.k_nbo, 1)
     for i, (a, b) in enumerate(CHUNKS):
         v.wait_ge(S["c%d" % i], 16)
-        v.quantize_mx(T.cq[:, a:b], T.cp[:, a:b], T.cb[:, 4 * a:4 * b]).then_inc(S.qc, 1)
-        if i == 1:
-            v.wait_ge(S.ul, 128)
-            v.tensor_copy(T.uo[:], T.ui[:]).then_inc(S.k_uo, 1)
+        v.quantize_mx(T.cq[:, a:b], T.cp[:, a:b], T.cb[:, 4 * a:4 * b]).then_inc(S.qc if i else S.qa, 1)
+        if i == 0:
+            spread(T.uo, T.ui, 32, S.ul, S.k_uo)
     far, own = (1 - host) * UO, host * UO
     for i, (a, b) in enumerate(PIECES):
-        pick("u%d" % i, "u", a, b, "c", T.uo[:, far + a // 16:far + b // 16], [("qc", len(CHUNKS)), ("k_uo", 1)] if i == 0 else [])
+        pick("u%d" % i, "u", a, b, "c", T.uo[:, far + a // 16:far + b // 16],
+             [("qa", 1), ("k_uo", 4), ("qc", len(CHUNKS) - 1)] if i == 0 else [])
     pick("v", "v", 0, UN, "c", T.uo[:, own:own + UO])
-    pick("n", "n", 0, CR, "v", T.ln[:, 0:LO], [("a_ln", len(leave))], [("p_v", 1)])
-    pick("e", "e", 0, 2 * CR, "v", T.lx[:], [("a_lx", 2 * len(leave))])
-    pick("s", "s", 0, CR, "v", T.no[:, rank * LO:(rank + 1) * LO], [("k_no", 1)])
-    v.wait_ge(S.wl, 16)
-    v.quantize_mx(T.wq[:], T.wp[:], T.wb[:]).then_inc(S.qw, 1)
+    pick("s", "s", 0, CR, "v", T.no[:, rank * LO:(rank + 1) * LO], [("k_no", 2)], [("p_v", 1)])
     v.wait_ge(S.pl, 128)
     v.tensor_copy(T.po[:], T.pi[:]).then_inc(S.k_po, 1)
-    pick("l", "l", 0, 2 * CR, "r", T.ln[:, LO:3 * LO], [], [("a_r", 4 * len(leave))])
-    pick("m", "m", 0, 2 * CR, "r", T.mo[:], [("k_mo", 2)])
+    for i in range(2):
+        pick("e%d" % i, "e", i * CR, (i + 1) * CR, "v", T.lx[:, i * LO:(i + 1) * LO], [("a_lx%d" % i, len(leave))])
+    pick("n", "n", 0, CR, "v", T.ln[:, 0:LO], [("a_ln", len(stay))])
+    v.wait_ge(S.wl, 16)
+    v.quantize_mx(T.wq[:], T.wp[:], T.wb[:]).then_inc(S.qw, 1)
+    for i in HELD:
+        v.wait_ge(S["a_r%dq" % i], len(PIECES) * len(leave))
+        sc.wait_ge(S["a_r%dp" % i], len(leave))
+        pick("l%d" % i, "l", i * CR, (i + 1) * CR, "r%d" % i, T.ln[:, (i + 1) * LO:(i + 2) * LO])
+    for i, q in enumerate((twin, other)):
+        pick("m%d" % i, "m", i * CR, (i + 1) * CR, "r%d" % i, T.no[:, q * LO:(q + 1) * LO])
 
     call, sent = _caller(g, core, T, topo)
-    g.wait_ge(S.k_no, 1)
-    call([(hands[i], T.lh[:], T.no[:, q * LO:(q + 1) * LO], S.a_lh, leave[i * half:(i + 1) * half]) for i, q in enumerate(cross)])
+    g.wait_ge(S.k_no, 2)
+    call([(hands[i], T.lh[:], T.no[:, q * LO:(q + 1) * LO], S.a_lh, (leave, stay)[i][:half]) for i, q in enumerate(cross[::-1])])
     g.wait_ge(S.k_nbo, 3)
-    call([(cores[nb], T.ln[:], T.nbo[:], S.a_ln, leave)])
+    call([(cores[nb], T.ln[:], T.nbo[:], S.a_ln, leave[half:] + stay[half:])])
+    for i, (a, b) in enumerate(PIECES):
+        g.wait_ge(S["p_u%dq" % i], 1)
+        call([(away[i], _view(T.xq, "q", a, b), _view(T.uq, "q", a, b), S.a_xq, leave)])
+        if i == 0:
+            for k in range(len(PIECES)):
+                g.wait_ge(S["p_u%dp" % k], 1)
+            call([(away[1], T.xp[:], T.up[:], S.a_xp, leave)])
+    for i in range(2):
+        g.wait_ge(S["p_e%dq" % i], 1)
+        call([(hands[i], _view(T.hq, "q", 0, CR), _view(T.eq, "q", i * CR, (i + 1) * CR), S.a_hq, (leave, chip)[i])])
+    for i in range(2):
+        g.wait_ge(S["p_e%dp" % i], 1)
+    call([(hands[i], T.hp[:], T.ep[:, i * CR:(i + 1) * CR], S.a_hp, (leave, stay)[i]) for i in range(2)])
     for s in "qp":
-        for i, (a, b) in enumerate(PIECES):
-            g.wait_ge(S["p_u%d%s" % (i, s)], 1)
-            call([(away[i], _view(T["x" + s], s, a, b), _view(T["u" + s], s, a, b), S["a_x" + s], leave)])
-
-    def columns(name, land, n):
-        for s in "qp":
-            g.wait_ge(S["p_" + name + s], 1)
-            call([(cores[nb], _view(T[land + s], s, 0, n), _view(T[name + s], s, 0, n), S["a_" + land + s], chip)])
-
-    columns("n", "f", CR)
-    for s in "qp":
-        g.wait_ge(S["p_e" + s], 1)
-        call([(hands[i], _view(T["h" + s], s, 0, CR), _view(T["e" + s], s, i * CR, (i + 1) * CR), S["a_h" + s],
-               chip[i * len(chip) // 2:(i + 1) * len(chip) // 2]) for i in range(2)])
-    columns("l", "t", 2 * CR)
+        g.wait_ge(S["p_n" + s], 1)
+        call([(cores[nb], _view(T["f" + s], s, 0, CR), _view(T["n" + s], s, 0, CR), S["a_f" + s], chip)])
+    for i in HELD:
+        g.wait_ge(S["p_l%dp" % i], 1)
+    call([(cores[nb], T.tp[:], T.lp[:], S.a_tp, chip)])
+    for i in HELD:
+        g.wait_ge(S["p_l%dq" % i], 1)
+        call([(cores[nb], _view(T.tq, "q", i * CR, (i + 1) * CR), _view(T.lq, "q", i * CR, (i + 1) * CR), S["a_t%d" % i], chip)])
     g.wait_ge(S.sent, sent[0])
 
     te.wait_ge(S.qw, 1)
 
-    def mm(i, name, a, b, waits=()):
+    def mm(i, name, at, waits=()):
         for s, n in waits:
             te.wait_ge(S[s], n)
-        te.matmul_mx(T.ps[:, 512 * i:512 * i + b - a], T.wq[:], T.wp[:], T[name + "q"][:, a:b], T[name + "p"][:, a:b], True, True).then_inc(S["mm%d" % i], 1)
+        a, b = at * CR, (at + 1) * CR
+        te.matmul_mx(T.ps[:, 512 * i:512 * i + CR], T.wq[:], T.wp[:], T[name + "q"][:, a:b], T[name + "p"][:, a:b], True, True).then_inc(S["mm%d" % i], 1)
 
-    mm(0, "s", 0, CR, [("p_sq", 1), ("p_sp", 1)])
-    mm(1, "f", 0, CR, [("a_fq", len(chip)), ("a_fp", len(chip))])
-    mm(2, "m", 0, 2 * CR, [("p_mq", 1), ("p_mp", 1)])
-    mm(3, "ek", 0, CR, [("a_ekq", 2 * len(leave)), ("a_ekp", 2 * len(leave))])
-    mm(4, "ek", CR, 2 * CR)
-    mm(5, "t", 0, CR, [("a_tq", len(chip)), ("a_tp", len(chip))])
-    mm(6, "t", CR, 2 * CR)
+    mm(0, "s", 0, [("p_sq", 1), ("p_sp", 1)])
+    mm(1, "f", 0, [("a_fq", len(chip)), ("a_fp", len(chip))])
+    mm(2, "m", 0, [("p_m0q", 1), ("p_m0p", 1)])
+    mm(3, "m", 1, [("p_m1q", 1), ("p_m1p", 1)])
+    mm(6, "t", 0, [("a_tp", len(chip)), ("a_t0", len(chip))])
+    mm(7, "t", 1, [("a_t1", len(chip))])
+    mm(5, "ek", 1, [("a_k1", 2 * len(leave))])
+    mm(4, "ek", 0, [("a_k0", 2 * len(leave))])
 
-    def zv(i, at, q):
-        v.wait_ge(S["mm%d" % i], 1)
-        v.tensor_copy(T.z[:, q * CR:(q + 1) * CR], T.ps[:, 512 * i + at * CR:512 * i + (at + 1) * CR]).then_inc(S.zv, 1)
+    zs(0, rank)
+    zs(1, nb)
+    zs(2, twin)
+    zs(3, other)
+    zs(6, nbrel[2])
+    zv(7, nbrel[3])
+    zs(5, cross[1])
+    zv(4, cross[0])
 
-    def zs(i, at, q):
-        sc.wait_ge(S["mm%d" % i], 1)
-        sc.activation(T.z[:, q * CR:(q + 1) * CR], T.ps[:, 512 * i + at * CR:512 * i + (at + 1) * CR], COPY).then_inc(S.zs, 1)
-
-    zv(0, 0, rank)
-    zs(1, 0, nb)
-    zv(2, 0, twin)
-    zv(2, 1, other)
-    zv(3, 0, cross[0])
-    zs(4, 0, cross[1])
-    zv(5, 0, nbrel[2])
-    zs(6, 0, nbrel[3])
     for q in (v, sc):
         q.wait_ge(S.k_po, 1)
-        q.wait_ge(S.zv, 5)
-        q.wait_ge(S.zs, 3)
-    for i, (a, b) in enumerate(YP):
-        offs = T.po[:, a // 16:b // 16]
-        if i % 2 == 0:
-            v.tensor_copy(T.yo[:, a:b], T.z[:].indirect(offs)).then_inc(S["g%d" % i], 1)
-        else:
-            sc.activation(T.yo[:, a:b], T.z[:].indirect(offs), COPY).then_inc(S["g%d" % i], 1)
-    for i, (a, b) in enumerate(YP):
-        sy.wait_ge(S["g%d" % i], 1)
-        sy.dma_start(T.y[:, a:b], T.yo[:, a:b]).then_inc(S.ystore, 16)
+        q.wait_ge(S.zv, 2)
+        q.wait_ge(S.zs, 6)
+    for i, (a, b, c) in enumerate(YP):
+        v.tensor_copy(T.yo[:, a:b], T.z[:].indirect(T.po[:, a // 16:b // 16])).then_inc(S["g%d" % i], 1)
+        sc.activation(T.yo[:, b:c], T.z[:].indirect(T.po[:, b // 16:c // 16]), COPY).then_inc(S["g%d" % i], 1)
+    for i, (a, b, c) in enumerate(YP):
+        sy.wait_ge(S["g%d" % i], 2)
+        sy.dma_start(T.y[:, a:c], T.yo[:, a:c]).then_inc(S.ystore, 16)
     sy.wait_ge(S.ystore, 16 * len(YP))

from concourse.bass import DstId, RemoteDMATransfer
from concourse.mybir import dt, ActivationFunctionType

COPY = ActivationFunctionType.Copy
TC, W, UN, CR, N, WORLD = 1024, 768, 320, 128, 8, 256
F8, U8 = "float8_e4m3fn_x4", "uint8"
UO, LO = UN // 16, CR // 16
CHUNKS = [(0, 512), (512, 896), (896, 1024)]
PIECES = [(0, 160), (160, 320)]
HELD = (0, 1)
YP = [(0, 64, 128), (128, 288, 448), (448, 608, 768)]

SCRATCH = {
    "cb": ("sbuf", [128, 4 * TC], "bfloat16"), "wb": ("sbuf", [128, 512], "bfloat16"),
    "ui": ("sbuf", [128, 2 * UO], "int32"), "ni": ("sbuf", [128, N * LO], "int32"), "pi": ("sbuf", [128, W // 16], "int32"),
    "uo": ("sbuf", [128, 2 * UO], "uint16"), "no": ("sbuf", [128, N * LO], "uint16"), "po": ("sbuf", [128, W // 16], "uint16"),
    "nbo": ("sbuf", [128, 3 * LO], "uint16"),
    "ln": ("sbuf", [128, 3 * LO], "uint16"),
    "lx": ("sbuf", [128, 2 * LO], "uint16"),
    "lh": ("sbuf", [128, LO], "uint16"),
    "z": ("sbuf", [128, N * CR], "float32"), "yo": ("sbuf", [128, W], "float32"),
    "ps": ("psum", [128, 512 * N], "float32"),
}
for _n, _w in [("c", TC), ("w", 128),
               ("u", UN), ("v", UN),
               ("x", UN), ("h", CR),
               ("r0", UN), ("r1", UN),
               ("e", 2 * CR), ("ek", 2 * CR),
               ("n", CR), ("f", CR),
               ("s", CR),
               ("l", 2 * CR), ("t", 2 * CR),
               ("m", 2 * CR)]:
    SCRATCH[_n + "q"] = ("sbuf", [128, _w], F8)
    SCRATCH[_n + "p"] = ("sbuf", [128, _w], U8)

PICKS = ["u0", "u1", "v", "n", "e0", "e1", "s", "l0", "l1", "m0", "m1"]
SEMAPHORES = (["wl", "ul", "nl", "pl", "k_no", "k_nbo", "k_uo", "k_po", "qa", "qc", "qw", "sent", "ystore",
               "a_lh", "a_ln", "a_lx0", "a_lx1", "zv", "zs", "a_k0", "a_k1"]
              + ["c%d" % i for i in range(len(CHUNKS))]
              + [a + b for a in ("a_x", "a_h", "a_r0", "a_r1", "a_f") for b in "qp"] + ["a_t0", "a_t1", "a_tp"]
              + ["p_" + a + b for a in PICKS for b in "qp"]
              + ["mm%d" % i for i in range(N)] + ["g%d" % i for i in range(len(YP))])


def _mask(engines):
    m = 0
    for e in engines:
        m |= 1 << e
    return m


def _rel(topo, cores, r):
    c = cores[r]
    here = [k for k in range(N) if topo.host(cores[k]) == topo.host(c)]
    there = [k for k in range(N) if topo.host(cores[k]) != topo.host(c) and topo.die(cores[k]) == topo.die(c)]
    nb = [k for k in here if k != r and topo.chip(cores[k]) == topo.chip(c)][0]
    cross = sorted((k for k in here if topo.chip(cores[k]) != topo.chip(c)), key=lambda k: topo.die(cores[k]) == topo.die(c))
    twin = [k for k in there if topo.chip(cores[k]) == topo.chip(c)][0]
    other = [k for k in there if k != twin][0]
    return nb, cross, twin, other


def _hands(topo, cores, r):
    c = cores[r]
    far = cores[_rel(topo, cores, r)[1][0]]
    fit = [k for k in range(WORLD) if topo.die(k) == topo.die(c) and topo.may_write(k, far)]
    return [[k for k in fit if topo.mates(k, far)][0], [k for k in fit if k in topo.cores_of(c)][0]]


def _view(t, s, a, b):
    return t[:, a:b].bitcast(dt.uint8) if s == "q" else t[:, a:b]


def _caller(g, core, T, topo):
    sent = [0]

    def call(jobs):
        if len(jobs) == 1:
            d, out, src, sem, eng = jobs[0]
            rid, pid = topo.addr(d, core)
            g.remote_dma(out, src, sem, T.sem.sent, pid, rid, _mask(eng))
        else:
            tr = []
            for d, out, src, sem, eng in jobs:
                rid, pid = topo.addr(d, core)
                tr.append(RemoteDMATransfer(dst_ids=[DstId(rid=rid, pnc=pid)], dma_engine_mask=_mask(eng), remote_sem=sem,
                                            srcs=[src], dsts=[out]))
            g.remote_dma_fused(tr, local_sem=T.sem.sent)
        sent[0] += sum(len(j[4]) for j in jobs)

    return call, sent


def _hand_program(g, core, T, topo, r, i):
    cores, S = T.cores, T.sem
    me = cores[r]
    nb, cross, twin, other = _rel(topo, cores, r)
    call, sent = _caller(g, core, T, topo)
    far = cores[cross[1]]
    away = topo.engines(core, far)
    near = [e for e in topo.engines(core, me) if e not in away] or away
    g.wait_ge(S.a_lh, len(away) // 2)
    call([(cores[cross[1 - i]], T.lx[:, (1 - i) * LO:(2 - i) * LO], T.lh[:], S["a_lx%d" % (1 - i)], away)])
    for s, (a, b) in [("p", (0, UN))] * i + [("q", PIECES[i])]:
        g.wait_ge(S["a_x" + s], len(away))
        src = _view(T["x" + s], s, a, b)
        to_far = (far, _view(T["r1" + s], s, a, b), src, S["a_r1" + s], away)
        to_me = (me, _view(T["r0" + s], s, a, b), src, S["a_r0" + s], near)
        for part in ([[to_far, to_me]] if i else [[to_me], [to_far]]):
            call(part)
    for s, came in (("q", len(topo.engines(me, core))), ("p", len(away))):
        g.wait_ge(S["a_h" + s], came)
        call([(cores[cross[i]], _view(T["ek" + s], s, i * CR, (i + 1) * CR), _view(T["h" + s], s, 0, CR), S["a_k%d" % i], away)])
    g.wait_ge(S.sent, sent[0])


def rank_program(g, core, T, topo):
    rank = T.rank_of(core)
    cores = T.cores
    if rank is None:
        for r in range(N):
            hands = _hands(topo, cores, r)
            if core in hands:
                _hand_program(g, core, T, topo, r, hands.index(core))
        return
    v, sc, te, sy = g.vector, g.scalar, g.tensor, g.sync
    S = T.sem
    nb, cross, twin, other = _rel(topo, cores, rank)
    nbrel = _rel(topo, cores, nb)
    hands = _hands(topo, cores, rank)
    away = _hands(topo, cores, twin)
    host = 0 if topo.host(core) == topo.host(cores[0]) else 1
    leave = topo.engines(core, cores[twin])
    chip = topo.engines(core, cores[nb])
    stay = [e for e in chip if e not in leave]
    half = len(leave) // 2

    for k in range(4):
        (sy, sc)[k % 2].dma_start(T.ni[16 * k:16 * k + 16, :], T.need[:]).then_inc(S.nl, 16)
    for i, (a, b) in enumerate(CHUNKS):
        sy.dma_start(T.cb[:, 4 * a:4 * b], T.c[:, 4 * a:4 * b]).then_inc(S["c%d" % i], 16)
    for k in range(2):
        sc.dma_start(T.ui[16 * k:16 * k + 16, :], T.uni[:]).then_inc(S.ul, 16)
    for k in range(8):
        sy.dma_start(T.pi[16 * k:16 * k + 16, :], T.pos[:]).then_inc(S.pl, 16)
    sy.wait_ge(S.p_vq, 1)
    sy.dma_start(T.wb[:], T.w[:]).then_inc(S.wl, 16)

    def pick(name, out, a, b, win, offs, waits=(), own=(), sides="qp"):
        for s in sides:
            queue = v if s == "q" else sc
            for sem, n in list(waits) + [(k + s, n) for k, n in own]:
                queue.wait_ge(S[sem], n)
            if s == "q":
                made = v.tensor_copy(T[out + s][:, a:b].bitcast(dt.uint32), T[win + s][:].bitcast(dt.uint32).indirect(offs))
            else:
                made = sc.activation(T[out + s][:, a:b], T[win + s][:].indirect(offs), COPY)
            made.then_inc(S["p_" + name + s], 1)

    def spread(out, loaded, n, lsem, sem):
        v.wait_ge(lsem, n)
        for k in range(0, 128, n):
            v.tensor_copy(out[k:k + n, :], loaded[0:n, :]).then_inc(sem, 1)

    def zv(i, q):
        v.wait_ge(S["mm%d" % i], 1)
        v.tensor_copy(T.z[:, q * CR:(q + 1) * CR], T.ps[:, 512 * i:512 * i + CR]).then_inc(S.zv, 1)

    def zs(i, q):
        sc.wait_ge(S["mm%d" % i], 1)
        sc.activation(T.z[:, q * CR:(q + 1) * CR], T.ps[:, 512 * i:512 * i + CR], COPY).then_inc(S.zs, 1)

    spread(T.no, T.ni, 64, S.nl, S.k_no)
    v.wait_ge(S.k_no, 2)
    for at, q in enumerate((nb, nbrel[2], nbrel[3])):
        v.tensor_copy(T.nbo[:, at * LO:(at + 1) * LO], T.no[:, q * LO:(q + 1) * LO]).then_inc(S.k_nbo, 1)
    for i, (a, b) in enumerate(CHUNKS):
        v.wait_ge(S["c%d" % i], 16)
        v.quantize_mx(T.cq[:, a:b], T.cp[:, a:b], T.cb[:, 4 * a:4 * b]).then_inc(S.qc if i else S.qa, 1)
        if i == 0:
            spread(T.uo, T.ui, 32, S.ul, S.k_uo)
    far, own = (1 - host) * UO, host * UO
    for i, (a, b) in enumerate(PIECES):
        pick("u%d" % i, "u", a, b, "c", T.uo[:, far + a // 16:far + b // 16],
             [("qa", 1), ("k_uo", 4), ("qc", len(CHUNKS) - 1)] if i == 0 else [])
    pick("v", "v", 0, UN, "c", T.uo[:, own:own + UO])
    pick("s", "s", 0, CR, "v", T.no[:, rank * LO:(rank + 1) * LO], [("k_no", 2)], [("p_v", 1)])
    v.wait_ge(S.pl, 128)
    v.tensor_copy(T.po[:], T.pi[:]).then_inc(S.k_po, 1)
    for i in range(2):
        pick("e%d" % i, "e", i * CR, (i + 1) * CR, "v", T.lx[:, i * LO:(i + 1) * LO], [("a_lx%d" % i, len(leave))])
    pick("n", "n", 0, CR, "v", T.ln[:, 0:LO], [("a_ln", len(stay))])
    v.wait_ge(S.wl, 16)
    v.quantize_mx(T.wq[:], T.wp[:], T.wb[:]).then_inc(S.qw, 1)
    for i in HELD:
        v.wait_ge(S["a_r%dq" % i], len(PIECES) * len(leave))
        sc.wait_ge(S["a_r%dp" % i], len(leave))
        pick("l%d" % i, "l", i * CR, (i + 1) * CR, "r%d" % i, T.ln[:, (i + 1) * LO:(i + 2) * LO])
    for i, q in enumerate((twin, other)):
        pick("m%d" % i, "m", i * CR, (i + 1) * CR, "r%d" % i, T.no[:, q * LO:(q + 1) * LO])

    call, sent = _caller(g, core, T, topo)
    g.wait_ge(S.k_no, 2)
    call([(hands[i], T.lh[:], T.no[:, q * LO:(q + 1) * LO], S.a_lh, (leave, stay)[i][:half]) for i, q in enumerate(cross[::-1])])
    g.wait_ge(S.k_nbo, 3)
    call([(cores[nb], T.ln[:], T.nbo[:], S.a_ln, leave[half:] + stay[half:])])
    for i, (a, b) in enumerate(PIECES):
        g.wait_ge(S["p_u%dq" % i], 1)
        call([(away[i], _view(T.xq, "q", a, b), _view(T.uq, "q", a, b), S.a_xq, leave)])
        if i == 0:
            for k in range(len(PIECES)):
                g.wait_ge(S["p_u%dp" % k], 1)
            call([(away[1], T.xp[:], T.up[:], S.a_xp, leave)])
    for i in range(2):
        g.wait_ge(S["p_e%dq" % i], 1)
        call([(hands[i], _view(T.hq, "q", 0, CR), _view(T.eq, "q", i * CR, (i + 1) * CR), S.a_hq, (leave, chip)[i])])
    for i in range(2):
        g.wait_ge(S["p_e%dp" % i], 1)
    call([(hands[i], T.hp[:], T.ep[:, i * CR:(i + 1) * CR], S.a_hp, (leave, stay)[i]) for i in range(2)])
    for s in "qp":
        g.wait_ge(S["p_n" + s], 1)
        call([(cores[nb], _view(T["f" + s], s, 0, CR), _view(T["n" + s], s, 0, CR), S["a_f" + s], chip)])
    for i in HELD:
        g.wait_ge(S["p_l%dp" % i], 1)
    call([(cores[nb], T.tp[:], T.lp[:], S.a_tp, chip)])
    for i in HELD:
        g.wait_ge(S["p_l%dq" % i], 1)
        call([(cores[nb], _view(T.tq, "q", i * CR, (i + 1) * CR), _view(T.lq, "q", i * CR, (i + 1) * CR), S["a_t%d" % i], chip)])
    g.wait_ge(S.sent, sent[0])

    te.wait_ge(S.qw, 1)

    def mm(i, name, at, waits=()):
        for s, n in waits:
            te.wait_ge(S[s], n)
        a, b = at * CR, (at + 1) * CR
        te.matmul_mx(T.ps[:, 512 * i:512 * i + CR], T.wq[:], T.wp[:], T[name + "q"][:, a:b], T[name + "p"][:, a:b], True, True).then_inc(S["mm%d" % i], 1)

    mm(0, "s", 0, [("p_sq", 1), ("p_sp", 1)])
    mm(1, "f", 0, [("a_fq", len(chip)), ("a_fp", len(chip))])
    mm(2, "m", 0, [("p_m0q", 1), ("p_m0p", 1)])
    mm(3, "m", 1, [("p_m1q", 1), ("p_m1p", 1)])
    mm(6, "t", 0, [("a_tp", len(chip)), ("a_t0", len(chip))])
    mm(7, "t", 1, [("a_t1", len(chip))])
    mm(5, "ek", 1, [("a_k1", 2 * len(leave))])
    mm(4, "ek", 0, [("a_k0", 2 * len(leave))])

    zs(0, rank)
    zs(1, nb)
    zs(2, twin)
    zs(3, other)
    zs(6, nbrel[2])
    zv(7, nbrel[3])
    zs(5, cross[1])
    zv(4, cross[0])

    for q in (v, sc):
        q.wait_ge(S.k_po, 1)
        q.wait_ge(S.zv, 2)
        q.wait_ge(S.zs, 6)
    for i, (a, b, c) in enumerate(YP):
        v.tensor_copy(T.yo[:, a:b], T.z[:].indirect(T.po[:, a // 16:b // 16])).then_inc(S["g%d" % i], 1)
        sc.activation(T.yo[:, b:c], T.z[:].indirect(T.po[:, b // 16:c // 16]), COPY).then_inc(S["g%d" % i], 1)
    for i, (a, b, c) in enumerate(YP):
        sy.wait_ge(S["g%d" % i], 2)
        sy.dma_start(T.y[:, a:c], T.yo[:, a:c]).then_inc(S.ystore, 16)
    sy.wait_ge(S.ystore, 16 * len(YP))
